import numpy as np
import ml_dtypes


def mxq(x, axis, fmt="e4m3"):
    dtype, down = {"e4m3": (ml_dtypes.float8_e4m3fn, 7), "e5m2": (ml_dtypes.float8_e5m2, 14)}[fmt]
    v = np.moveaxis(np.asarray(x, np.float32).astype(ml_dtypes.bfloat16).astype(np.float64), axis, -1)
    blocks = v.reshape(v.shape[:-1] + (-1, 32))
    amax = np.abs(blocks).max(-1, keepdims=True)
    byte = np.maximum(np.where(amax > 0, np.frexp(amax)[1] - 1 + 127, 0) - down, 1)
    scale = np.exp2(byte - 127.0)
    codes = (blocks / scale).astype(np.float32).astype(dtype).astype(np.float64)
    return np.moveaxis((codes * scale).reshape(v.shape), -1, axis)


WIDE = False


def mx_kscale(k):
    if not WIDE:
        return np.ones(k)
    levels = np.array([10, -10, 5, -5, 0])
    if k % 512:
        return np.exp2(np.random.permutation(np.resize(levels, k // 32))).repeat(32)
    a = np.empty((k // 512, 16))
    for p in range(k // 512):
        a[p, :8] = np.random.permutation(np.resize(levels, 8))
        for g in range(8):
            far = levels[np.abs(levels - a[p, g]) >= 10]
            a[p, g + 8] = far[np.random.randint(len(far))]
    return np.exp2(a.ravel()).repeat(32)


def f64(x):
    return np.asarray(x).astype(np.float64)


def striped(idx):
    return np.tile(idx.reshape(-1, 16).T, (8, 1)).astype(np.uint16)


def unstriped(offs):
    return offs[:16].T.reshape(-1).astype(np.int64)


def striped8(idx):
    return np.concatenate([x.reshape(-1, 16).T for x in idx]).astype(np.uint16)


def runs(offs, k):
    lists = np.stack([offs[16 * r : 16 * r + 16].T.reshape(-1) for r in range(8)]).astype(np.int64)
    return lists[np.arange(k) % 512 // 64]


def pack_weight(w):
    k, n = w.shape
    w = f64(np.asarray(w, np.float32).astype(ml_dtypes.bfloat16)).reshape(k // 32, 32, n)
    amax = np.abs(w).max(1)
    byte = np.clip(np.where(amax > 0, np.frexp(amax)[1] - 1 + 127 - 7, 1), 1, 254)
    scaled = (w * np.exp2(127.0 - byte)[:, None, :]).reshape(k, n).astype(np.float32)
    words = np.ascontiguousarray(scaled.reshape(k // 512, 128, 4, n).transpose(0, 1, 3, 2)).astype(ml_dtypes.float8_e4m3fn).view(np.uint8)
    return words, np.ascontiguousarray(byte.astype(np.uint8).reshape(k // 512, 16, n))


def unpack_weight(words, scales):
    g, p, n, _ = words.shape
    vals = np.ascontiguousarray(words).view(ml_dtypes.float8_e4m3fn).astype(np.float64) * np.repeat(np.exp2(scales.astype(np.float64) - 127.0), 8, axis=1)[..., None]
    return vals.transpose(0, 1, 3, 2).reshape(g * 512, n)


K, T, S, H, W, G, U = 512, 2048, 256, 512, 128, 2048, 1024


def setup_inputs():
    n = np.random.standard_normal
    s = mx_kscale(K)[:, None]
    packed_xT = pack_weight(n((K, T)) * s)
    packed_dT = pack_weight(n((K, G)) / s)
    perm = np.random.permutation(S)
    return {
        "x_words": packed_xT[0],
        "x_scales": packed_xT[1],
        "w1": (n((K, H)) / np.sqrt(K) / s).astype(np.float32),
        "gs": (np.random.uniform(0.5, 1.5, (K, 1)) * s).astype(np.float32),
        "d_words": packed_dT[0],
        "d_scales": packed_dT[1],
        "mem": n((H, U)).astype(np.float32),
        "offs": striped8(np.random.randint(0, T, (8, S))),
        "n1": striped(perm[:W]),
        "n2": striped(perm[W:]),
        "ka": striped8(np.random.randint(0, G, (8, H))),
        "kb": striped8(np.random.randint(0, G, (8, H))),
        "n3": striped(np.random.permutation(U)[:S]),
    }


def reference(x_words, x_scales, w1, gs, d_words, d_scales, mem, offs, n1, n2, ka, kb, n3):
    d_ka = unpack_weight(d_words, d_scales)[np.arange(K)[:, None], runs(ka, K)]
    xq = unpack_weight(x_words, x_scales)[np.arange(K)[:, None], runs(offs, K)]
    y = mxq(f64(w1), 0, "e4m3").T @ xq
    pb = y[:, unstriped(n2)]
    pa = y[:, unstriped(n1)]
    rb = pb - (0.5 * pa)
    ra = np.sqrt((pa) ** 2 + (pb) ** 2 + 0.25)
    ds = np.zeros((H, S))
    ds[:, unstriped(n1)] = ra
    dt = ds.copy()
    dt[:, unstriped(n2)] = rb
    z = f64(gs) * dt
    zq = mxq(z, 0, "e4m3")
    d_kb = unpack_weight(d_words, d_scales)[np.arange(K)[:, None], runs(kb, K)]
    h = 0.0625 * (d_ka.T @ zq + d_kb.T @ zq)
    out = f64(mem).copy()
    out[:, unstriped(n3)] = h
    return out

@@ -1,0 +1,164 @@
+from contextlib import ExitStack
+
+import concourse.mybir as mybir
+
+F32 = mybir.dt.float32
+BF16 = mybir.dt.bfloat16
+I32 = mybir.dt.int32
+U32 = mybir.dt.uint32
+U16 = mybir.dt.uint16
+U8 = mybir.dt.uint8
+FP8X4 = mybir.dt.float8_e4m3fn_x4
+ALU = mybir.AluOpType
+ACT = mybir.ActivationFunctionType
+
+P = 128
+K, T, S, H, W, G, U = 512, 2048, 256, 512, 128, 2048, 1024
+FLOPS = 2 * K * H * S * 3
+
+
+def tile_picked_hdaqpolarpage_none_p_kernel(
+    tc, x_words, x_scales, w1, gs, d_words, d_scales, mem, offs, n1, n2, ka, kb, n3, out
+):
+    nc = tc.nc
+    with ExitStack() as ctx:
+        keep = ctx.enter_context(tc.tile_pool(name="keep", bufs=1))
+        work = ctx.enter_context(tc.tile_pool(name="work", bufs=1))
+        psum = ctx.enter_context(tc.psum_pool(name="psum", bufs=1))
+
+        def load_list(src, name):
+            tile = keep.tile(list(src.shape), U16, name=name)
+            nc.sync.dma_start(tile[:], src)
+            return tile
+
+        def load_scale_rows(queue, src, name):
+            tile = work.tile([P, src.shape[2]], U8, name=name, align_bytes=64)
+            nc.gpsimd.memset(tile[:].bitcast(I32), 0)
+            queue.dma_start(tile[0:P:8, :].bitcast(I32), src[0].bitcast(I32))
+            return tile
+
+        def load_words(src, name, tag):
+            tile = work.tile([P, src.shape[2]], U32, name=name, tag=tag, align_bytes=64)
+            nc.sync.dma_start(tile[:].bitcast(I32), src[0].rearrange("p n t -> p (n t)").bitcast(I32))
+            return tile
+
+        def place_scale_rows(queue, plane, picked):
+            for q in range(4):
+                queue.dma_start(plane[32 * q : 32 * q + 4, :].bitcast(I32), picked[32 * q : 32 * q + 32 : 8, :].bitcast(I32))
+
+        offs_t = load_list(offs, "offs_t")
+        w_raw = work.tile([P, 4, H], F32, name="w_raw", align_bytes=64)
+        nc.sync.dma_start(w_raw[:], w1.rearrange("(p j) c -> p j c", j=4))
+        n1_t = load_list(n1, "n1_t")
+        n2_t = load_list(n2, "n2_t")
+        ka_t = load_list(ka, "ka_t")
+        kb_t = load_list(kb, "kb_t")
+        n3_t = load_list(n3, "n3_t")
+        xw_table = load_words(x_words, "xw_table", "xw_table")
+        xs_table = load_scale_rows(nc.scalar, x_scales, "xs_table")
+        ds_table = load_scale_rows(nc.sync, d_scales, "ds_table")
+
+        x_plane = work.tile([P, S], U8, name="x_plane", align_bytes=64)
+        nc.vector.memset(x_plane[:].bitcast(I32), 0)
+        d_plane = work.tile([P, 2 * H], U8, name="d_plane", align_bytes=64)
+        nc.vector.memset(d_plane[:].bitcast(I32), 0)
+
+        xs_picked = work.tile([P, S], U8, name="xs_picked")
+        nc.vector.tensor_copy(xs_picked[:], xs_table[:].indirect(offs_t[:]))
+        place_scale_rows(nc.sync, x_plane, xs_picked)
+
+        w_bf = work.tile([P, 4, P, 4], BF16, name="w_bf", align_bytes=64)
+        for copy, lo, hi in ((nc.vector.tensor_copy, 0, 80), (nc.scalar.copy, 80, P)):
+            copy(
+                w_bf[:, :, lo:hi, :].rearrange("p t m j -> p m j t"),
+                w_raw[:, :, 4 * lo : 4 * hi].rearrange("p j (m t) -> p m j t", t=4),
+            )
+        dw_table = load_words(d_words, "dw_table", "w_raw")
+        w_codes = work.tile([P, H], U32, name="w_codes", align_bytes=64)
+        w_plane = work.tile([P, H], U8, name="w_plane", align_bytes=64)
+        nc.vector.quantize_mx(out=w_codes[:].bitcast(FP8X4), scales=w_plane[:], in_=w_bf[:].rearrange("p t m j -> p (t m j)"))
+
+        x_codes = work.tile([P, S], U32, name="x_codes", align_bytes=64)
+        nc.vector.tensor_copy(x_codes[:], xw_table[:].indirect(offs_t[:]))
+
+
+        ys = []
+        for t in range(4):
+            acc = psum.tile([P, S], F32, name=f"y_acc{t}", tag=f"bank{t}")
+            cols = slice(P * t, P * (t + 1))
+            nc.tensor.matmul_mx(out=acc[:], lhsT=w_codes[:, cols].bitcast(FP8X4), lhsT_scale=w_plane[:, cols],
+                                rhs=x_codes[:].bitcast(FP8X4), rhs_scale=x_plane[:], start=True, stop=True)
+            y = work.tile([P, S], F32, name=f"y{t}", align_bytes=64)
+            nc.vector.tensor_copy(y[:], acc[:])
+            ys.append(y)
+
+        pairs = work.tile([P, 4, 2, W], F32, name="pairs")
+        rb = work.tile([P, 4, W], F32, name="rb")
+        ds_picked = work.tile([P, 2 * H], U8, name="ds_picked", tag="w_plane", align_bytes=64)
+
+        def pick_d_scales(u):
+            lst = (ka_t, kb_t)[u // 2]
+            nc.vector.tensor_copy(ds_picked[:, 256 * u : 256 * (u + 1)], ds_table[:].indirect(lst[:, 16 * (u % 2) : 16 * (u % 2 + 1)]))
+
+        for t in range(4):
+            nc.scalar.activation(pairs[:, t, 0, :], ys[t][:].indirect(n1_t[:]), ACT.Copy)
+            nc.scalar.activation(pairs[:, t, 1, :], ys[t][:].indirect(n2_t[:]), ACT.Copy)
+            nc.vector.scalar_tensor_tensor(rb[:, t, :], pairs[:, t, 0, :], -0.5, pairs[:, t, 1, :], ALU.mult, ALU.add)
+            if t in (1, 2):
+                pick_d_scales(t - 1)
+        gs_t = work.tile([P, 4], F32, name="gs_t", tag="xs_picked")
+        nc.sync.dma_start(gs_t[:], gs.rearrange("(p t) o -> p (t o)", t=4))
+        pages = []
+        for b, tag in enumerate(("w_bf", "xw_table", "w_codes", "x_codes")):
+            page = work.tile([P, U], F32, name=f"page{b}", tag=tag, align_bytes=64)
+            nc.sync.dma_start(page[:], mem[P * b : P * (b + 1), :])
+            pages.append(page)
+        squares = work.tile([P, 4, 2, W], F32, name="squares", align_bytes=64)
+        radicand = work.tile([P, 4, W], F32, name="radicand")
+        for u in range(2):
+            two = slice(2 * u, 2 * u + 2)
+            nc.vector.tensor_tensor(squares[:, two], pairs[:, two], pairs[:, two], ALU.mult)
+        for u in range(2):
+            two = slice(2 * u, 2 * u + 2)
+            nc.vector.scalar_tensor_tensor(radicand[:, two], squares[:, two, 0, :], 0.25, squares[:, two, 1, :], ALU.add, ALU.add)
+        pick_d_scales(2)
+        pick_d_scales(3)
+        place_scale_rows(nc.sync, d_plane, ds_picked)
+        dts = []
+        for t in range(4):
+            dt = work.tile([P, S], F32, name=f"dt{t}", tag=f"y{3 - t}", align_bytes=64)
+            nc.scalar.activation(dt[:].indirect(n2_t[:]), rb[:, t, :], ACT.Copy)
+            dts.append(dt)
+        ra = work.tile([P, 4, W], F32, name="ra")
+        for u in range(2):
+            nc.scalar.activation(ra[:, 2 * u : 2 * u + 2, :], radicand[:, 2 * u : 2 * u + 2, :], ACT.Sqrt)
+
+        d_codes = work.tile([P, 2 * H], U32, name="d_codes", tag="squares", align_bytes=64)
+        for u in range(4):
+            lst = (ka_t, kb_t)[u // 2]
+            nc.vector.tensor_copy(d_codes[:, 256 * u : 256 * (u + 1)], dw_table[:].indirect(lst[:, 16 * (u % 2) : 16 * (u % 2 + 1)]))
+
+        z_bf = work.tile([P, S, 4], BF16, name="z_bf", align_bytes=64)
+        for t in range(4):
+            nc.scalar.activation(dts[t][:].indirect(n1_t[:]), ra[:, t, :], ACT.Copy)
+            for cols in ([slice(0, S)] if t < 3 else [slice(0, P), slice(P, S)]):
+                nc.vector.tensor_scalar(z_bf[:, cols, t], dts[t][:, cols], gs_t[:, t : t + 1], None, ALU.mult)
+
+        z_codes = work.tile([P, S], U32, name="z_codes", align_bytes=64)
+        z_plane = work.tile([P, S], U8, name="z_plane", align_bytes=64)
+        for cols in (slice(0, P), slice(P, S)):
+            nc.vector.quantize_mx(out=z_codes[:, cols].bitcast(FP8X4), scales=z_plane[:, cols], in_=z_bf[:, cols, :].rearrange("p s t -> p (s t)"))
+
+        pieces = [(0, 0, P), (0, P, S), (1, 0, S), (2, 0, S), (3, 0, S)]
+        for i, (b, lo, hi) in enumerate(pieces):
+            acc = psum.tile([P, hi - lo], F32, name=f"h_acc{i}", tag=f"bank{(4 + i) % 8}")
+            for side in range(2):
+                rows = slice(H * side + P * b, H * side + P * (b + 1))
+                nc.tensor.matmul_mx(out=acc[:], lhsT=d_codes[:, rows].bitcast(FP8X4),
+                                    lhsT_scale=d_plane[:, rows],
+                                    rhs=z_codes[:, lo:hi].bitcast(FP8X4), rhs_scale=z_plane[:, lo:hi], start=(side == 0), stop=(side == 1))
+            h = work.tile([P, hi - lo], F32, name=f"h{i}")
+            nc.vector.tensor_scalar(h[:], acc[:], 0.0625, None, ALU.mult)
+            nc.scalar.activation(pages[b][:].indirect(n3_t[:, lo // 16 : hi // 16]), h[:], ACT.Copy)
+            if hi == S:
+                nc.sync.dma_start(out[P * b : P * (b + 1), :], pages[b][:])

@@ -56,6 +56,9 @@ def tile_picked_hdaqpolarpage_none_p_kernel(
         n3_t = load_list(n3, "n3_t")
         xw_table = load_words(x_words, "xw_table", "xw_table")
         xs_table = load_scale_rows(nc.scalar, x_scales, "xs_table")
+        warm = work.tile([P, 2], F32, name="warm")
+        nc.gpsimd.memset(warm[:, 0:1], 1.0)
+        nc.scalar.activation(warm[:, 1:2], warm[:, 0:1], ACT.Sqrt)
         ds_table = load_scale_rows(nc.sync, d_scales, "ds_table")
 
         x_plane = work.tile([P, S], U8, name="x_plane", align_bytes=64)

@@ -31,9 +31,9 @@ def tile_picked_hdaqpolarpage_none_p_kernel(
             nc.sync.dma_start(tile[:], src)
             return tile
 
-        def load_scale_rows(queue, src, name):
-            tile = work.tile([P, src.shape[2]], U8, name=name, align_bytes=64)
-            nc.gpsimd.memset(tile[:].bitcast(I32), 0)
+        def load_scale_rows(queue, clear, src, name):
+            tile = work.tile([P, src.shape[2]], U8, name=name, tag="scale_table", align_bytes=64)
+            clear.memset(tile[:].bitcast(I32), 0)
             queue.dma_start(tile[0:P:8, :].bitcast(I32), src[0].bitcast(I32))
             return tile
 
@@ -52,14 +52,13 @@ def tile_picked_hdaqpolarpage_none_p_kernel(
         n1_t = load_list(n1, "n1_t")
         n2_t = load_list(n2, "n2_t")
         ka_t = load_list(ka, "ka_t")
+        xw_table = load_words(x_words, "xw_table", "xw_table")
         kb_t = load_list(kb, "kb_t")
         n3_t = load_list(n3, "n3_t")
-        xw_table = load_words(x_words, "xw_table", "xw_table")
-        xs_table = load_scale_rows(nc.scalar, x_scales, "xs_table")
+        xs_table = load_scale_rows(nc.scalar, nc.vector, x_scales, "xs_table")
         warm = work.tile([P, 2], F32, name="warm")
-        nc.gpsimd.memset(warm[:, 0:1], 1.0)
+        nc.vector.memset(warm[:, 0:1], 1.0)
         nc.scalar.activation(warm[:, 1:2], warm[:, 0:1], ACT.Sqrt)
-        ds_table = load_scale_rows(nc.sync, d_scales, "ds_table")
 
         x_plane = work.tile([P, S], U8, name="x_plane", align_bytes=64)
         nc.vector.memset(x_plane[:].bitcast(I32), 0)
@@ -69,6 +68,8 @@ def tile_picked_hdaqpolarpage_none_p_kernel(
         xs_picked = work.tile([P, S], U8, name="xs_picked")
         nc.vector.tensor_copy(xs_picked[:], xs_table[:].indirect(offs_t[:]))
         place_scale_rows(nc.sync, x_plane, xs_picked)
+
+        ds_table = load_scale_rows(nc.sync, nc.gpsimd, d_scales, "ds_table")
 
         w_bf = work.tile([P, 4, P, 4], BF16, name="w_bf", align_bytes=64)
         for copy, lo, hi in ((nc.vector.tensor_copy, 0, 80), (nc.scalar.copy, 80, P)):

from contextlib import ExitStack

import concourse.mybir as mybir

F32 = mybir.dt.float32
BF16 = mybir.dt.bfloat16
I32 = mybir.dt.int32
U32 = mybir.dt.uint32
U16 = mybir.dt.uint16
U8 = mybir.dt.uint8
FP8X4 = mybir.dt.float8_e4m3fn_x4
ALU = mybir.AluOpType
ACT = mybir.ActivationFunctionType

P = 128
K, T, S, H, W, G, U = 512, 2048, 256, 512, 128, 2048, 1024
FLOPS = 2 * K * H * S * 3


def tile_picked_hdaqpolarpage_none_p_kernel(
    tc, x_words, x_scales, w1, gs, d_words, d_scales, mem, offs, n1, n2, ka, kb, n3, out
):
    nc = tc.nc
    with ExitStack() as ctx:
        keep = ctx.enter_context(tc.tile_pool(name="keep", bufs=1))
        work = ctx.enter_context(tc.tile_pool(name="work", bufs=1))
        psum = ctx.enter_context(tc.psum_pool(name="psum", bufs=1))

        def load_list(src, name):
            tile = keep.tile(list(src.shape), U16, name=name)
            nc.sync.dma_start(tile[:], src)
            return tile

        def load_scale_rows(queue, clear, src, name):
            tile = work.tile([P, src.shape[2]], U8, name=name, tag="scale_table", align_bytes=64)
            clear.memset(tile[:].bitcast(I32), 0)
            queue.dma_start(tile[0:P:8, :].bitcast(I32), src[0].bitcast(I32))
            return tile

        def load_words(src, name, tag):
            tile = work.tile([P, src.shape[2]], U32, name=name, tag=tag, align_bytes=64)
            nc.sync.dma_start(tile[:].bitcast(I32), src[0].rearrange("p n t -> p (n t)").bitcast(I32))
            return tile

        def place_scale_rows(queue, plane, picked):
            for q in range(4):
                queue.dma_start(plane[32 * q : 32 * q + 4, :].bitcast(I32), picked[32 * q : 32 * q + 32 : 8, :].bitcast(I32))

        offs_t = load_list(offs, "offs_t")
        w_raw = work.tile([P, 4, H], F32, name="w_raw", align_bytes=64)
        nc.sync.dma_start(w_raw[:], w1.rearrange("(p j) c -> p j c", j=4))
        n1_t = load_list(n1, "n1_t")
        n2_t = load_list(n2, "n2_t")
        ka_t = load_list(ka, "ka_t")
        xw_table = load_words(x_words, "xw_table", "xw_table")
        kb_t = load_list(kb, "kb_t")
        n3_t = load_list(n3, "n3_t")
        xs_table = load_scale_rows(nc.scalar, nc.vector, x_scales, "xs_table")
        warm = work.tile([P, 2], F32, name="warm")
        nc.vector.memset(warm[:, 0:1], 1.0)
        nc.scalar.activation(warm[:, 1:2], warm[:, 0:1], ACT.Sqrt)

        x_plane = work.tile([P, S], U8, name="x_plane", align_bytes=64)
        nc.vector.memset(x_plane[:].bitcast(I32), 0)
        d_plane = work.tile([P, 2 * H], U8, name="d_plane", align_bytes=64)
        nc.vector.memset(d_plane[:].bitcast(I32), 0)

        xs_picked = work.tile([P, S], U8, name="xs_picked")
        nc.vector.tensor_copy(xs_picked[:], xs_table[:].indirect(offs_t[:]))
        place_scale_rows(nc.sync, x_plane, xs_picked)

        ds_table = load_scale_rows(nc.sync, nc.gpsimd, d_scales, "ds_table")

        w_bf = work.tile([P, 4, P, 4], BF16, name="w_bf", align_bytes=64)
        for copy, lo, hi in ((nc.vector.tensor_copy, 0, 80), (nc.scalar.copy, 80, P)):
            copy(
                w_bf[:, :, lo:hi, :].rearrange("p t m j -> p m j t"),
                w_raw[:, :, 4 * lo : 4 * hi].rearrange("p j (m t) -> p m j t", t=4),
            )
        dw_table = load_words(d_words, "dw_table", "w_raw")
        w_codes = work.tile([P, H], U32, name="w_codes", align_bytes=64)
        w_plane = work.tile([P, H], U8, name="w_plane", align_bytes=64)
        nc.vector.quantize_mx(out=w_codes[:].bitcast(FP8X4), scales=w_plane[:], in_=w_bf[:].rearrange("p t m j -> p (t m j)"))

        x_codes = work.tile([P, S], U32, name="x_codes", align_bytes=64)
        nc.vector.tensor_copy(x_codes[:], xw_table[:].indirect(offs_t[:]))


        ys = []
        for t in range(4):
            acc = psum.tile([P, S], F32, name=f"y_acc{t}", tag=f"bank{t}")
            cols = slice(P * t, P * (t + 1))
            nc.tensor.matmul_mx(out=acc[:], lhsT=w_codes[:, cols].bitcast(FP8X4), lhsT_scale=w_plane[:, cols],
                                rhs=x_codes[:].bitcast(FP8X4), rhs_scale=x_plane[:], start=True, stop=True)
            y = work.tile([P, S], F32, name=f"y{t}", align_bytes=64)
            nc.vector.tensor_copy(y[:], acc[:])
            ys.append(y)

        pairs = work.tile([P, 4, 2, W], F32, name="pairs")
        rb = work.tile([P, 4, W], F32, name="rb")
        ds_picked = work.tile([P, 2 * H], U8, name="ds_picked", tag="w_plane", align_bytes=64)

        def pick_d_scales(u):
            lst = (ka_t, kb_t)[u // 2]
            nc.vector.tensor_copy(ds_picked[:, 256 * u : 256 * (u + 1)], ds_table[:].indirect(lst[:, 16 * (u % 2) : 16 * (u % 2 + 1)]))

        for t in range(4):
            nc.scalar.activation(pairs[:, t, 0, :], ys[t][:].indirect(n1_t[:]), ACT.Copy)
            nc.scalar.activation(pairs[:, t, 1, :], ys[t][:].indirect(n2_t[:]), ACT.Copy)
            nc.vector.scalar_tensor_tensor(rb[:, t, :], pairs[:, t, 0, :], -0.5, pairs[:, t, 1, :], ALU.mult, ALU.add)
            if t in (1, 2):
                pick_d_scales(t - 1)
        gs_t = work.tile([P, 4], F32, name="gs_t", tag="xs_picked")
        nc.sync.dma_start(gs_t[:], gs.rearrange("(p t) o -> p (t o)", t=4))
        pages = []
        for b, tag in enumerate(("w_bf", "xw_table", "w_codes", "x_codes")):
            page = work.tile([P, U], F32, name=f"page{b}", tag=tag, align_bytes=64)
            nc.sync.dma_start(page[:], mem[P * b : P * (b + 1), :])
            pages.append(page)
        squares = work.tile([P, 4, 2, W], F32, name="squares", align_bytes=64)
        radicand = work.tile([P, 4, W], F32, name="radicand")
        for u in range(2):
            two = slice(2 * u, 2 * u + 2)
            nc.vector.tensor_tensor(squares[:, two], pairs[:, two], pairs[:, two], ALU.mult)
        for u in range(2):
            two = slice(2 * u, 2 * u + 2)
            nc.vector.scalar_tensor_tensor(radicand[:, two], squares[:, two, 0, :], 0.25, squares[:, two, 1, :], ALU.add, ALU.add)
        pick_d_scales(2)
        pick_d_scales(3)
        place_scale_rows(nc.sync, d_plane, ds_picked)
        dts = []
        for t in range(4):
            dt = work.tile([P, S], F32, name=f"dt{t}", tag=f"y{3 - t}", align_bytes=64)
            nc.scalar.activation(dt[:].indirect(n2_t[:]), rb[:, t, :], ACT.Copy)
            dts.append(dt)
        ra = work.tile([P, 4, W], F32, name="ra")
        for u in range(2):
            nc.scalar.activation(ra[:, 2 * u : 2 * u + 2, :], radicand[:, 2 * u : 2 * u + 2, :], ACT.Sqrt)

        d_codes = work.tile([P, 2 * H], U32, name="d_codes", tag="squares", align_bytes=64)
        for u in range(4):
            lst = (ka_t, kb_t)[u // 2]
            nc.vector.tensor_copy(d_codes[:, 256 * u : 256 * (u + 1)], dw_table[:].indirect(lst[:, 16 * (u % 2) : 16 * (u % 2 + 1)]))

        z_bf = work.tile([P, S, 4], BF16, name="z_bf", align_bytes=64)
        for t in range(4):
            nc.scalar.activation(dts[t][:].indirect(n1_t[:]), ra[:, t, :], ACT.Copy)
            for cols in ([slice(0, S)] if t < 3 else [slice(0, P), slice(P, S)]):
                nc.vector.tensor_scalar(z_bf[:, cols, t], dts[t][:, cols], gs_t[:, t : t + 1], None, ALU.mult)

        z_codes = work.tile([P, S], U32, name="z_codes", align_bytes=64)
        z_plane = work.tile([P, S], U8, name="z_plane", align_bytes=64)
        for cols in (slice(0, P), slice(P, S)):
            nc.vector.quantize_mx(out=z_codes[:, cols].bitcast(FP8X4), scales=z_plane[:, cols], in_=z_bf[:, cols, :].rearrange("p s t -> p (s t)"))

        pieces = [(0, 0, P), (0, P, S), (1, 0, S), (2, 0, S), (3, 0, S)]
        for i, (b, lo, hi) in enumerate(pieces):
            acc = psum.tile([P, hi - lo], F32, name=f"h_acc{i}", tag=f"bank{(4 + i) % 8}")
            for side in range(2):
                rows = slice(H * side + P * b, H * side + P * (b + 1))
                nc.tensor.matmul_mx(out=acc[:], lhsT=d_codes[:, rows].bitcast(FP8X4),
                                    lhsT_scale=d_plane[:, rows],
                                    rhs=z_codes[:, lo:hi].bitcast(FP8X4), rhs_scale=z_plane[:, lo:hi], start=(side == 0), stop=(side == 1))
            h = work.tile([P, hi - lo], F32, name=f"h{i}")
            nc.vector.tensor_scalar(h[:], acc[:], 0.0625, None, ALU.mult)
            nc.scalar.activation(pages[b][:].indirect(n3_t[:, lo // 16 : hi // 16]), h[:], ACT.Copy)
            if hi == S:
                nc.sync.dma_start(out[P * b : P * (b + 1), :], pages[b][:])
